import numpy as np, ml_dtypes
CORES = [74,78,202,206,330,334,458,462]
N = 8
COUNTS = [[0,64,0,0,0,0,32,64],[256,0,32,64,32,0,64,64],[256,0,0,32,32,0,64,64],[256,0,32,0,64,0,0,64],[256,0,0,32,0,0,32,64],[256,0,32,64,0,0,64,64],[256,32,64,0,0,0,0,64],[256,32,64,64,0,64,0,0]]
XW, YW = 512, 1792
def setup_inputs(rng):
    return {"x": rng.standard_normal((N, 128, XW), dtype=np.float32).astype(ml_dtypes.bfloat16)}
def reference(x):
    y = np.full((N, 128, YW), np.nan, x.dtype)
    fill = [0] * N
    for s in range(N):
        o = 0
        for d in range(N):
            c = COUNTS[s][d]
            y[d][:, fill[d]:fill[d] + c] = x[s][:, o:o + c]
            o += c; fill[d] += c
    return {"y": y}

@@ -1,0 +1,157 @@
+from concourse.bass import DstId, RemoteDMATransfer
+
+BF = "bfloat16"
+SCRATCH = {
+    "xs": ("sbuf", [128, 512], BF),
+    "land": ("sbuf", [128, 1792], BF),
+    "sd256": ("dram", [1, 128, 256], BF),
+    "sd64": ("dram", [3, 128, 64], BF),
+    "sd32": ("dram", [1, 128, 32], BF),
+    "ld256": ("dram", [2, 128, 256], BF),
+    "ld64": ("dram", [1, 128, 64], BF),
+    "ld32": ("dram", [1, 128, 32], BF),
+}
+SEMAPHORES = ["ldd", "lds", "sent", "st", "arr", "arr2", "arr3", "arr4"]
+
+PASS = {
+    (4, 0): (3, 0), (5, 0): (3, 4),
+    (1, 4): (3, 3),
+    (2, 6): (2, 1), (2, 7): (2, 5), (3, 7): (2, 7),
+    (6, 2): (2, 0), (7, 2): (2, 4), (7, 3): (2, 3),
+}
+LONE = {(7, 5)}
+SENDS = {
+    0: [[(1, 0xFF00), (7, 0x00FF)], [(6, 0x00FF)]],
+    1: [[(4, 0x00FF)], [(0, 0xFF00)], [(3, 0x000F), (6, 0x0030), (7, 0x00C0)], [(2, 0x000F)]],
+    2: [[(6, 0x000F), (7, 0x00F0)], [(0, 0x00FF)], [(3, 0xFF00), (4, 0x00FF)]],
+    3: [[(7, 0x00FF)], [(0, 0x00FF)], [(4, 0x00FF)], [(2, 0xFF00)]],
+    4: [[(0, 0x00FF)], [(7, 0x00FF)], [(3, 0x000F), (6, 0x00F0)]],
+    5: [[(0, 0x00FF)], [(3, 0x000F), (6, 0x0030), (7, 0x00C0)], [(2, 0x000F)]],
+    6: [[(2, 0x00FF), (7, 0xFF00)], [(0, 0x00FF)], [(1, 0x00FF)]],
+    7: [[(2, 0x000F), (3, 0x0030), (5, 0x00C0)], [(0, 0x00FF)], [(1, 0x00FF)]],
+}
+SEM0 = {1: "arr", 2: "arr", 3: "arr", 6: "arr2", 7: "arr2", 4: "arr3", 5: "arr4"}
+
+
+def bits(m):
+    return bin(m).count("1")
+
+
+def make_plan(T):
+    C = T.tables["COUNTS"]
+    cores = list(T.cores)
+    n = len(cores)
+    xoff = [[sum(C[s][:d]) for d in range(n)] for s in range(n)]
+    yoff = [[sum(C[k][d] for k in range(s)) for s in range(n)] for d in range(n)]
+    loads = {c: [] for c in cores}
+    calls = {}
+    expect = {}
+    stores = {c: [] for c in cores}
+
+    def add(core, sem, k):
+        expect[(core, sem)] = expect.get((core, sem), 0) + k
+
+    for s in range(n):
+        me = cores[s]
+        calls[me] = []
+        slot = {}
+        lo, hi = None, None
+        for call in SENDS[s]:
+            trs, need = [], set()
+            for d, m in call:
+                w = C[s][d]
+                a = xoff[s][d]
+                final_sem = SEM0[s] if d == 0 else "arr"
+                if (s, d) in PASS or (s, d) in LONE:
+                    k = slot.get(w, 0)
+                    slot[w] = k + 1
+                    src = ("sd%d" % w, k)
+                    loads[me].append(("sync", "ldd", src, a, a + w))
+                    add(me, "ldd", 16)
+                    need.add("ldd")
+                    if d == 0:
+                        fin = ("ld%d" % w, s - 4)
+                        stores[cores[0]].append((final_sem, fin, yoff[d][s], yoff[d][s] + w))
+                    elif (s, d) in LONE:
+                        fin = ("ld%d" % w, 0)
+                        stores[cores[d]].append((final_sem, fin, yoff[d][s], yoff[d][s] + w))
+                    else:
+                        fin = ("land", yoff[d][s], yoff[d][s] + w)
+                    if (s, d) in PASS:
+                        h, c = PASS[(s, d)]
+                        hc = h * 128 + (me % 128) - (me % 8) + c
+                        trs.append((src, hc, ("ld%d" % w, 0), m, "arr"))
+                        add(hc, "arr", bits(m))
+                        calls[hc] = [({"arr"}, [(("ld%d" % w, 0), cores[d], fin, 0x00FF, final_sem)])]
+                        add(cores[d], final_sem, 8)
+                        add(hc, "sent", 8)
+                    else:
+                        trs.append((src, cores[d], fin, m, final_sem))
+                        add(cores[d], final_sem, bits(m))
+                else:
+                    lo = a if lo is None else min(lo, a)
+                    hi = a + w if hi is None else max(hi, a + w)
+                    need.add("lds")
+                    trs.append((("xs", a, a + w), cores[d], ("land", yoff[d][s], yoff[d][s] + w), m, final_sem))
+                    add(cores[d], final_sem, bits(m))
+                add(me, "sent", bits(m))
+            calls[me].append((need, trs))
+        if lo is not None:
+            loads[me].append(("scalar", "lds", ("xs", lo, hi), lo, hi))
+            add(me, "lds", 16)
+    for d in range(n):
+        runs = {}
+        for s in range(n):
+            if C[s][d] and not (d == 0 and (s, d) in PASS) and (s, d) not in LONE:
+                sem = SEM0[s] if d == 0 else "arr"
+                a, b = yoff[d][s], yoff[d][s] + C[s][d]
+                if sem in runs:
+                    runs[sem] = (min(runs[sem][0], a), max(runs[sem][1], b))
+                else:
+                    runs[sem] = (a, b)
+        for sem in runs:
+            a, b = runs[sem]
+            stores[cores[d]].append((sem, ("land", a, b), a, b))
+    return loads, calls, expect, stores
+
+
+def ap(T, desc):
+    if len(desc) == 3:
+        return T[desc[0]][:, desc[1]:desc[2]]
+    return T[desc[0]][desc[1]]
+
+
+def rank_program(g, core, T, topo):
+    loads, calls, expect, stores = make_plan(T)
+    if core not in calls:
+        return
+    queue = {"sync": g.sync, "scalar": g.scalar}
+    for q, sem, dst, a, b in loads.get(core, []):
+        queue[q].dma_start(ap(T, dst), T.x[:, a:b]).then_inc(T.sem[sem], 16)
+    order = {"arr": 0, "arr2": 1, "arr3": 2, "arr4": 3}
+    mine = sorted(stores.get(core, []), key=lambda t: order[t[0]])
+    for i, (sem, src, a, b) in enumerate(mine):
+        q = g.sync if i % 2 == 0 else g.scalar
+        q.wait_ge(T.sem[sem], expect[(core, sem)])
+        q.dma_start(T.y[:, a:b], ap(T, src)).then_inc(T.sem.st, 16)
+    waited = set()
+    for need, trs in calls[core]:
+        for sem in sorted(need):
+            if sem not in waited:
+                g.wait_ge(T.sem[sem], expect[(core, sem)])
+                waited.add(sem)
+        if len(trs) == 1:
+            src, dc, dst, m, sem = trs[0]
+            rid, pid = topo.addr(dc, core)
+            g.remote_dma(out_ap=ap(T, dst), in_ap=ap(T, src), remote_sem=T.sem[sem], local_sem=T.sem.sent,
+                         pid=pid, routing_id=rid, dma_engine_mask=m)
+        else:
+            lst = []
+            for src, dc, dst, m, sem in trs:
+                rid, pid = topo.addr(dc, core)
+                lst.append(RemoteDMATransfer(dst_ids=[DstId(rid=rid, pnc=pid)], dma_engine_mask=m,
+                                             remote_sem=T.sem[sem], src=ap(T, src), dst=ap(T, dst)))
+            g.remote_dma_fused(lst, local_sem=T.sem.sent)
+    g.wait_ge(T.sem.sent, expect[(core, "sent")])
+    if mine:
+        g.wait_ge(T.sem.st, 16 * len(mine))

@@ -4,21 +4,21 @@ BF = "bfloat16"
 SCRATCH = {
     "xs": ("sbuf", [128, 512], BF),
     "land": ("sbuf", [128, 1792], BF),
-    "sd256": ("dram", [1, 128, 256], BF),
+    "sdh": ("dram", [2, 128, 128], BF),
+    "ldh": ("dram", [4, 128, 128], BF),
     "sd64": ("dram", [3, 128, 64], BF),
     "sd32": ("dram", [1, 128, 32], BF),
-    "ld256": ("dram", [2, 128, 256], BF),
     "ld64": ("dram", [1, 128, 64], BF),
     "ld32": ("dram", [1, 128, 32], BF),
 }
 SEMAPHORES = ["ldd", "lds", "sent", "st", "arr", "arr2", "arr3", "arr4"]
 
 PASS = {
-    (4, 0): (3, 0), (5, 0): (3, 4),
     (1, 4): (3, 3),
     (2, 6): (2, 1), (2, 7): (2, 5), (3, 7): (2, 7),
     (6, 2): (2, 0), (7, 2): (2, 4), (7, 3): (2, 3),
 }
+HOT = {4: ((3, 0), (1, 0)), 5: ((3, 4), (1, 4))}
 LONE = {(7, 5)}
 SENDS = {
     0: [[(1, 0xFF00), (7, 0x00FF)], [(6, 0x00FF)]],
@@ -61,7 +61,24 @@ def make_plan(T):
             for d, m in call:
                 w = C[s][d]
                 a = xoff[s][d]
+                ya = yoff[d][s]
                 final_sem = SEM0[s] if d == 0 else "arr"
+                if d == 0 and s in HOT:
+                    loads[me].append(("sync", "ldd", ("sdh", 0, 2, None), a, a + w))
+                    add(me, "ldd", 16)
+                    need.add("ldd")
+                    i = s - 4
+                    for j, (h, c) in enumerate(HOT[s]):
+                        hc = h * 128 + (me % 128) - (me % 8) + c
+                        mj = (0x000F, 0x00F0)[j]
+                        trs.append((("sdh", j), hc, ("ldh", 0), mj, "arr"))
+                        add(hc, "arr", 4)
+                        add(me, "sent", 4)
+                        calls[hc] = [({"arr"}, [(("ldh", 0), cores[0], ("ldh", 2 * i + j), 0x00FF, final_sem)])]
+                        add(cores[0], final_sem, 8)
+                        add(hc, "sent", 8)
+                    stores[cores[0]].append((final_sem, ("ldh", 2 * i, 2 * i + 2, None), ya, ya + w))
+                    continue
                 if (s, d) in PASS or (s, d) in LONE:
                     k = slot.get(w, 0)
                     slot[w] = k + 1
@@ -69,14 +86,11 @@ def make_plan(T):
                     loads[me].append(("sync", "ldd", src, a, a + w))
                     add(me, "ldd", 16)
                     need.add("ldd")
-                    if d == 0:
-                        fin = ("ld%d" % w, s - 4)
-                        stores[cores[0]].append((final_sem, fin, yoff[d][s], yoff[d][s] + w))
-                    elif (s, d) in LONE:
+                    if (s, d) in LONE:
                         fin = ("ld%d" % w, 0)
-                        stores[cores[d]].append((final_sem, fin, yoff[d][s], yoff[d][s] + w))
+                        stores[cores[d]].append((final_sem, fin, ya, ya + w))
                     else:
-                        fin = ("land", yoff[d][s], yoff[d][s] + w)
+                        fin = ("land", ya, ya + w)
                     if (s, d) in PASS:
                         h, c = PASS[(s, d)]
                         hc = h * 128 + (me % 128) - (me % 8) + c
@@ -92,7 +106,7 @@ def make_plan(T):
                     lo = a if lo is None else min(lo, a)
                     hi = a + w if hi is None else max(hi, a + w)
                     need.add("lds")
-                    trs.append((("xs", a, a + w), cores[d], ("land", yoff[d][s], yoff[d][s] + w), m, final_sem))
+                    trs.append((("xs", a, a + w), cores[d], ("land", ya, ya + w), m, final_sem))
                     add(cores[d], final_sem, bits(m))
                 add(me, "sent", bits(m))
             calls[me].append((need, trs))
@@ -102,7 +116,7 @@ def make_plan(T):
     for d in range(n):
         runs = {}
         for s in range(n):
-            if C[s][d] and not (d == 0 and (s, d) in PASS) and (s, d) not in LONE:
+            if C[s][d] and not (d == 0 and s in HOT) and (s, d) not in LONE:
                 sem = SEM0[s] if d == 0 else "arr"
                 a, b = yoff[d][s], yoff[d][s] + C[s][d]
                 if sem in runs:
@@ -116,6 +130,8 @@ def make_plan(T):
 
 
 def ap(T, desc):
+    if len(desc) == 4:
+        return T[desc[0]][desc[1]:desc[2]]
     if len(desc) == 3:
         return T[desc[0]][:, desc[1]:desc[2]]
     return T[desc[0]][desc[1]]

@@ -19,18 +19,19 @@ PASS = {
     (6, 2): (2, 0), (7, 2): (2, 4), (7, 3): (2, 3),
 }
 HOT = {4: ((3, 0), (1, 0)), 5: ((3, 4), (1, 4))}
-LONE = {(7, 5)}
+LONE = {(7, 5), (3, 4)}
 SENDS = {
     0: [[(1, 0xFF00), (7, 0x00FF)], [(6, 0x00FF)]],
-    1: [[(4, 0x00FF)], [(0, 0xFF00)], [(3, 0x000F), (6, 0x0030), (7, 0x00C0)], [(2, 0x000F)]],
+    1: [[(4, 0x000C), (2, 0x0003)], [(0, 0xFF00)], [(3, 0x000C), (6, 0x0030), (7, 0x00C0)]],
     2: [[(6, 0x000F), (7, 0x00F0)], [(0, 0x00FF)], [(3, 0xFF00), (4, 0x00FF)]],
-    3: [[(7, 0x00FF)], [(0, 0x00FF)], [(4, 0x00FF)], [(2, 0xFF00)]],
+    3: [[(7, 0x000F), (4, 0x00F0)], [(0, 0x00FF)], [(2, 0xFF00)]],
     4: [[(0, 0x00FF)], [(7, 0x00FF)], [(3, 0x000F), (6, 0x00F0)]],
     5: [[(0, 0x00FF)], [(3, 0x000F), (6, 0x0030), (7, 0x00C0)], [(2, 0x000F)]],
     6: [[(2, 0x00FF), (7, 0xFF00)], [(0, 0x00FF)], [(1, 0x00FF)]],
     7: [[(2, 0x000F), (3, 0x0030), (5, 0x00C0)], [(0, 0x00FF)], [(1, 0x00FF)]],
 }
 SEM0 = {1: "arr", 2: "arr", 3: "arr", 6: "arr2", 7: "arr2", 4: "arr3", 5: "arr4"}
+TURN = ("sync", "scalar")
 
 
 def bits(m):
@@ -62,7 +63,7 @@ def make_plan(T):
                 w = C[s][d]
                 a = xoff[s][d]
                 ya = yoff[d][s]
-                final_sem = SEM0[s] if d == 0 else "arr"
+                final_sem = SEM0[s] if d == 0 else ("arr2" if (s, d) in LONE else "arr")
                 if d == 0 and s in HOT:
                     loads[me].append(("sync", "ldd", ("sdh", 0, 2, None), a, a + w))
                     add(me, "ldd", 16)
@@ -83,7 +84,7 @@ def make_plan(T):
                     k = slot.get(w, 0)
                     slot[w] = k + 1
                     src = ("sd%d" % w, k)
-                    loads[me].append(("sync", "ldd", src, a, a + w))
+                    loads[me].append((TURN[len(loads[me]) % 2], "ldd", src, a, a + w))
                     add(me, "ldd", 16)
                     need.add("ldd")
                     if (s, d) in LONE:
@@ -111,7 +112,7 @@ def make_plan(T):
                 add(me, "sent", bits(m))
             calls[me].append((need, trs))
         if lo is not None:
-            loads[me].append(("scalar", "lds", ("xs", lo, hi), lo, hi))
+            loads[me].append((TURN[len(loads[me]) % 2], "lds", ("xs", lo, hi), lo, hi))
             add(me, "lds", 16)
     for d in range(n):
         runs = {}

from concourse.bass import DstId, RemoteDMATransfer

BF = "bfloat16"
SCRATCH = {
    "xs": ("sbuf", [128, 512], BF),
    "land": ("sbuf", [128, 1792], BF),
    "sdh": ("dram", [2, 128, 128], BF),
    "ldh": ("dram", [4, 128, 128], BF),
    "sd64": ("dram", [3, 128, 64], BF),
    "sd32": ("dram", [1, 128, 32], BF),
    "ld64": ("dram", [1, 128, 64], BF),
    "ld32": ("dram", [1, 128, 32], BF),
}
SEMAPHORES = ["ldd", "lds", "sent", "st", "arr", "arr2", "arr3", "arr4"]

PASS = {
    (1, 4): (3, 3),
    (2, 6): (2, 1), (2, 7): (2, 5), (3, 7): (2, 7),
    (6, 2): (2, 0), (7, 2): (2, 4), (7, 3): (2, 3),
}
HOT = {4: ((3, 0), (1, 0)), 5: ((3, 4), (1, 4))}
LONE = {(7, 5), (3, 4)}
SENDS = {
    0: [[(1, 0xFF00), (7, 0x00FF)], [(6, 0x00FF)]],
    1: [[(4, 0x000C), (2, 0x0003)], [(0, 0xFF00)], [(3, 0x000C), (6, 0x0030), (7, 0x00C0)]],
    2: [[(6, 0x000F), (7, 0x00F0)], [(0, 0x00FF)], [(3, 0xFF00), (4, 0x00FF)]],
    3: [[(7, 0x000F), (4, 0x00F0)], [(0, 0x00FF)], [(2, 0xFF00)]],
    4: [[(0, 0x00FF)], [(7, 0x00FF)], [(3, 0x000F), (6, 0x00F0)]],
    5: [[(0, 0x00FF)], [(3, 0x000F), (6, 0x0030), (7, 0x00C0)], [(2, 0x000F)]],
    6: [[(2, 0x00FF), (7, 0xFF00)], [(0, 0x00FF)], [(1, 0x00FF)]],
    7: [[(2, 0x000F), (3, 0x0030), (5, 0x00C0)], [(0, 0x00FF)], [(1, 0x00FF)]],
}
SEM0 = {1: "arr", 2: "arr", 3: "arr", 6: "arr2", 7: "arr2", 4: "arr3", 5: "arr4"}
TURN = ("sync", "scalar")


def bits(m):
    return bin(m).count("1")


def make_plan(T):
    C = T.tables["COUNTS"]
    cores = list(T.cores)
    n = len(cores)
    xoff = [[sum(C[s][:d]) for d in range(n)] for s in range(n)]
    yoff = [[sum(C[k][d] for k in range(s)) for s in range(n)] for d in range(n)]
    loads = {c: [] for c in cores}
    calls = {}
    expect = {}
    stores = {c: [] for c in cores}

    def add(core, sem, k):
        expect[(core, sem)] = expect.get((core, sem), 0) + k

    for s in range(n):
        me = cores[s]
        calls[me] = []
        slot = {}
        lo, hi = None, None
        for call in SENDS[s]:
            trs, need = [], set()
            for d, m in call:
                w = C[s][d]
                a = xoff[s][d]
                ya = yoff[d][s]
                final_sem = SEM0[s] if d == 0 else ("arr2" if (s, d) in LONE else "arr")
                if d == 0 and s in HOT:
                    loads[me].append(("sync", "ldd", ("sdh", 0, 2, None), a, a + w))
                    add(me, "ldd", 16)
                    need.add("ldd")
                    i = s - 4
                    for j, (h, c) in enumerate(HOT[s]):
                        hc = h * 128 + (me % 128) - (me % 8) + c
                        mj = (0x000F, 0x00F0)[j]
                        trs.append((("sdh", j), hc, ("ldh", 0), mj, "arr"))
                        add(hc, "arr", 4)
                        add(me, "sent", 4)
                        calls[hc] = [({"arr"}, [(("ldh", 0), cores[0], ("ldh", 2 * i + j), 0x00FF, final_sem)])]
                        add(cores[0], final_sem, 8)
                        add(hc, "sent", 8)
                    stores[cores[0]].append((final_sem, ("ldh", 2 * i, 2 * i + 2, None), ya, ya + w))
                    continue
                if (s, d) in PASS or (s, d) in LONE:
                    k = slot.get(w, 0)
                    slot[w] = k + 1
                    src = ("sd%d" % w, k)
                    loads[me].append((TURN[len(loads[me]) % 2], "ldd", src, a, a + w))
                    add(me, "ldd", 16)
                    need.add("ldd")
                    if (s, d) in LONE:
                        fin = ("ld%d" % w, 0)
                        stores[cores[d]].append((final_sem, fin, ya, ya + w))
                    else:
                        fin = ("land", ya, ya + w)
                    if (s, d) in PASS:
                        h, c = PASS[(s, d)]
                        hc = h * 128 + (me % 128) - (me % 8) + c
                        trs.append((src, hc, ("ld%d" % w, 0), m, "arr"))
                        add(hc, "arr", bits(m))
                        calls[hc] = [({"arr"}, [(("ld%d" % w, 0), cores[d], fin, 0x00FF, final_sem)])]
                        add(cores[d], final_sem, 8)
                        add(hc, "sent", 8)
                    else:
                        trs.append((src, cores[d], fin, m, final_sem))
                        add(cores[d], final_sem, bits(m))
                else:
                    lo = a if lo is None else min(lo, a)
                    hi = a + w if hi is None else max(hi, a + w)
                    need.add("lds")
                    trs.append((("xs", a, a + w), cores[d], ("land", ya, ya + w), m, final_sem))
                    add(cores[d], final_sem, bits(m))
                add(me, "sent", bits(m))
            calls[me].append((need, trs))
        if lo is not None:
            loads[me].append((TURN[len(loads[me]) % 2], "lds", ("xs", lo, hi), lo, hi))
            add(me, "lds", 16)
    for d in range(n):
        runs = {}
        for s in range(n):
            if C[s][d] and not (d == 0 and s in HOT) and (s, d) not in LONE:
                sem = SEM0[s] if d == 0 else "arr"
                a, b = yoff[d][s], yoff[d][s] + C[s][d]
                if sem in runs:
                    runs[sem] = (min(runs[sem][0], a), max(runs[sem][1], b))
                else:
                    runs[sem] = (a, b)
        for sem in runs:
            a, b = runs[sem]
            stores[cores[d]].append((sem, ("land", a, b), a, b))
    return loads, calls, expect, stores


def ap(T, desc):
    if len(desc) == 4:
        return T[desc[0]][desc[1]:desc[2]]
    if len(desc) == 3:
        return T[desc[0]][:, desc[1]:desc[2]]
    return T[desc[0]][desc[1]]


def rank_program(g, core, T, topo):
    loads, calls, expect, stores = make_plan(T)
    if core not in calls:
        return
    queue = {"sync": g.sync, "scalar": g.scalar}
    for q, sem, dst, a, b in loads.get(core, []):
        queue[q].dma_start(ap(T, dst), T.x[:, a:b]).then_inc(T.sem[sem], 16)
    order = {"arr": 0, "arr2": 1, "arr3": 2, "arr4": 3}
    mine = sorted(stores.get(core, []), key=lambda t: order[t[0]])
    for i, (sem, src, a, b) in enumerate(mine):
        q = g.sync if i % 2 == 0 else g.scalar
        q.wait_ge(T.sem[sem], expect[(core, sem)])
        q.dma_start(T.y[:, a:b], ap(T, src)).then_inc(T.sem.st, 16)
    waited = set()
    for need, trs in calls[core]:
        for sem in sorted(need):
            if sem not in waited:
                g.wait_ge(T.sem[sem], expect[(core, sem)])
                waited.add(sem)
        if len(trs) == 1:
            src, dc, dst, m, sem = trs[0]
            rid, pid = topo.addr(dc, core)
            g.remote_dma(out_ap=ap(T, dst), in_ap=ap(T, src), remote_sem=T.sem[sem], local_sem=T.sem.sent,
                         pid=pid, routing_id=rid, dma_engine_mask=m)
        else:
            lst = []
            for src, dc, dst, m, sem in trs:
                rid, pid = topo.addr(dc, core)
                lst.append(RemoteDMATransfer(dst_ids=[DstId(rid=rid, pnc=pid)], dma_engine_mask=m,
                                             remote_sem=T.sem[sem], src=ap(T, src), dst=ap(T, dst)))
            g.remote_dma_fused(lst, local_sem=T.sem.sent)
    g.wait_ge(T.sem.sent, expect[(core, "sent")])
    if mine:
        g.wait_ge(T.sem.st, 16 * len(mine))
